import numpy as np
import ml_dtypes

BF16 = ml_dtypes.bfloat16


def bf(x):
    return np.asarray(x, np.float32).astype(BF16)


def f32(x):
    return np.asarray(x, np.float32)


def f64(x):
    return np.asarray(x).astype(np.float64)


def striped(idx):
    return np.concatenate([l.reshape(-1, 16).T for l in idx])


def rows(idx, k):
    return np.tile(np.repeat(idx, 16, axis=0), (k // (16 * 8), 1))


def look(tab, idx):
    return np.take_along_axis(f64(tab), rows(idx, len(tab)), axis=1)


K, S, V, N = 128, 2048, 1024, 1024


def setup_inputs():
    return {"tab": f32(np.random.standard_normal((2, K, S))), "y": f32(np.random.standard_normal((K, V))), "offs": striped(np.stack([np.random.permutation(S)[:N] for _ in range(8)]))}


def reference(tab, y, offs):
    idx = np.stack([g.T.reshape(-1) for g in np.split(offs, 8)])
    x = (look(tab[0], idx) * f64(y)) * (1.0 / (1.0 + np.exp(-look(tab[1], idx))))
    return x

@@ -1,0 +1,52 @@
+import concourse.mybir as mybir
+
+F32, U16 = mybir.dt.float32, mybir.dt.uint16
+SIGMOID = mybir.ActivationFunctionType.Sigmoid
+MULT = mybir.AluOpType.mult
+
+P = 128
+ENTRIES_A_COLUMN = 16
+GATE_PIECE = 512
+VALUE_PIECE = 256
+
+
+def entries(offsets, start, count):
+    return offsets[:, start // ENTRIES_A_COLUMN : (start + count) // ENTRIES_A_COLUMN]
+
+
+def tile_lookup_vg_mulsig_out_kernel(tc, tab, y, offs, out):
+    nc = tc.nc
+    places = tab.shape[2]
+    n = y.shape[1]
+    with (
+        tc.tile_pool(name="held", bufs=1) as held,
+        tc.tile_pool(name="work", bufs=2) as work,
+        tc.tile_pool(name="results", bufs=4) as results,
+    ):
+        offsets = held.tile([P, n // ENTRIES_A_COLUMN], U16)
+        gates = held.tile([P, places], F32)
+        stream = held.tile([P, n], F32)
+        values = held.tile([P, places], F32)
+
+        warm_up = held.tile([P, 1], F32)
+        nc.vector.memset(warm_up[:], 0.0)
+        warmed = held.tile([P, 1], F32)
+        nc.scalar.activation(warmed[:], warm_up[:], SIGMOID)
+
+        nc.sync.dma_start(offsets[:], offs)
+        nc.sync.dma_start(gates[:], tab[1])
+        nc.sync.dma_start(stream[:], y)
+        nc.sync.dma_start(values[:], tab[0])
+
+        gated_stream = held.tile([P, n], F32)
+        for start in range(0, n, GATE_PIECE):
+            columns = slice(start, start + GATE_PIECE)
+            opened = work.tile([P, GATE_PIECE], F32)
+            nc.scalar.activation(opened[:], gates[:].indirect(entries(offsets, start, GATE_PIECE)), SIGMOID)
+            nc.vector.tensor_tensor(gated_stream[:, columns], opened[:], stream[:, columns], MULT)
+        for start in range(0, n, VALUE_PIECE):
+            columns = slice(start, start + VALUE_PIECE)
+            result = results.tile([P, VALUE_PIECE], F32)
+            piece = entries(offsets, start, VALUE_PIECE)
+            nc.vector.tensor_tensor(result[:], values[:].indirect(piece), gated_stream[:, columns], MULT)
+            nc.sync.dma_start(out[:, columns], result[:])

@@ -7,46 +7,41 @@ MULT = mybir.AluOpType.mult
 P = 128
 ENTRIES_A_COLUMN = 16
 GATE_PIECE = 512
-VALUE_PIECE = 256
+VALUE_CUTS = (0, 384, 640, 896, 1024)
 
 
-def entries(offsets, start, count):
-    return offsets[:, start // ENTRIES_A_COLUMN : (start + count) // ENTRIES_A_COLUMN]
+def entries(offsets, start, stop):
+    return offsets[:, start // ENTRIES_A_COLUMN : stop // ENTRIES_A_COLUMN]
 
 
 def tile_lookup_vg_mulsig_out_kernel(tc, tab, y, offs, out):
     nc = tc.nc
     places = tab.shape[2]
     n = y.shape[1]
-    with (
-        tc.tile_pool(name="held", bufs=1) as held,
-        tc.tile_pool(name="work", bufs=2) as work,
-        tc.tile_pool(name="results", bufs=4) as results,
-    ):
+    with tc.tile_pool(name="held", bufs=1) as held:
         offsets = held.tile([P, n // ENTRIES_A_COLUMN], U16)
         gates = held.tile([P, places], F32)
         stream = held.tile([P, n], F32)
         values = held.tile([P, places], F32)
+        opened = held.tile([P, n], F32)
+        gated_stream = held.tile([P, n], F32)
+        result = held.tile([P, n], F32)
 
         warm_up = held.tile([P, 1], F32)
         nc.vector.memset(warm_up[:], 0.0)
         warmed = held.tile([P, 1], F32)
         nc.scalar.activation(warmed[:], warm_up[:], SIGMOID)
 
-        nc.sync.dma_start(offsets[:], offs)
         nc.sync.dma_start(gates[:], tab[1])
+        nc.sync.dma_start(offsets[:], offs)
         nc.sync.dma_start(stream[:], y)
         nc.sync.dma_start(values[:], tab[0])
 
-        gated_stream = held.tile([P, n], F32)
         for start in range(0, n, GATE_PIECE):
-            columns = slice(start, start + GATE_PIECE)
-            opened = work.tile([P, GATE_PIECE], F32)
-            nc.scalar.activation(opened[:], gates[:].indirect(entries(offsets, start, GATE_PIECE)), SIGMOID)
-            nc.vector.tensor_tensor(gated_stream[:, columns], opened[:], stream[:, columns], MULT)
-        for start in range(0, n, VALUE_PIECE):
-            columns = slice(start, start + VALUE_PIECE)
-            result = results.tile([P, VALUE_PIECE], F32)
-            piece = entries(offsets, start, VALUE_PIECE)
-            nc.vector.tensor_tensor(result[:], values[:].indirect(piece), gated_stream[:, columns], MULT)
-            nc.sync.dma_start(out[:, columns], result[:])
+            stop = start + GATE_PIECE
+            nc.scalar.activation(opened[:, start:stop], gates[:].indirect(entries(offsets, start, stop)), SIGMOID)
+            nc.vector.tensor_tensor(gated_stream[:, start:stop], opened[:, start:stop], stream[:, start:stop], MULT)
+        for start, stop in zip(VALUE_CUTS, VALUE_CUTS[1:]):
+            looked_up = values[:].indirect(entries(offsets, start, stop))
+            nc.vector.tensor_tensor(result[:, start:stop], looked_up, gated_stream[:, start:stop], MULT)
+            nc.sync.dma_start(out[:, start:stop], result[:, start:stop])

@@ -7,7 +7,7 @@ MULT = mybir.AluOpType.mult
 P = 128
 ENTRIES_A_COLUMN = 16
 GATE_PIECE = 512
-VALUE_CUTS = (0, 384, 640, 896, 1024)
+VALUE_CUTS = (0, 384, 704, 896, 1024)
 
 
 def entries(offsets, start, stop):

@@ -7,7 +7,9 @@ MULT = mybir.AluOpType.mult
 P = 128
 ENTRIES_A_COLUMN = 16
 GATE_PIECE = 512
-VALUE_CUTS = (0, 384, 704, 896, 1024)
+EARLY = 256
+UNGATED = 704
+LAST_PIECE = 192
 
 
 def entries(offsets, start, stop):
@@ -24,24 +26,41 @@ def tile_lookup_vg_mulsig_out_kernel(tc, tab, y, offs, out):
         stream = held.tile([P, n], F32)
         values = held.tile([P, places], F32)
         opened = held.tile([P, n], F32)
-        gated_stream = held.tile([P, n], F32)
+        partial = held.tile([P, n], F32)
         result = held.tile([P, n], F32)
-
-        warm_up = held.tile([P, 1], F32)
-        nc.vector.memset(warm_up[:], 0.0)
-        warmed = held.tile([P, 1], F32)
-        nc.scalar.activation(warmed[:], warm_up[:], SIGMOID)
 
         nc.sync.dma_start(gates[:], tab[1])
         nc.sync.dma_start(offsets[:], offs)
-        nc.sync.dma_start(stream[:], y)
+        nc.sync.dma_start(stream[:, :EARLY], y[:, :EARLY])
         nc.sync.dma_start(values[:], tab[0])
+        nc.sync.dma_start(stream[:, EARLY:], y[:, EARLY:])
+
+        def look_up(into, factor, start, stop):
+            looked_up = values[:].indirect(entries(offsets, start, stop))
+            nc.vector.tensor_tensor(into[:, start:stop], looked_up, factor[:, start:stop], MULT)
+
+        def gate(into, factor, start, stop):
+            nc.vector.tensor_tensor(into[:, start:stop], opened[:, start:stop], factor[:, start:stop], MULT)
+
+        def store(start, stop):
+            nc.sync.dma_start(out[:, start:stop], result[:, start:stop])
 
         for start in range(0, n, GATE_PIECE):
             stop = start + GATE_PIECE
             nc.scalar.activation(opened[:, start:stop], gates[:].indirect(entries(offsets, start, stop)), SIGMOID)
-            nc.vector.tensor_tensor(gated_stream[:, start:stop], opened[:, start:stop], stream[:, start:stop], MULT)
-        for start, stop in zip(VALUE_CUTS, VALUE_CUTS[1:]):
-            looked_up = values[:].indirect(entries(offsets, start, stop))
-            nc.vector.tensor_tensor(result[:, start:stop], looked_up, gated_stream[:, start:stop], MULT)
-            nc.sync.dma_start(out[:, start:stop], result[:, start:stop])
+
+        early_halves = ((0, EARLY // 2), (EARLY // 2, EARLY))
+        for start, stop in early_halves:
+            look_up(partial, stream, start, stop)
+        for start, stop in early_halves:
+            gate(result, partial, start, stop)
+        look_up(partial, stream, EARLY, GATE_PIECE)
+        look_up(partial, stream, GATE_PIECE, UNGATED)
+        gate(result, partial, EARLY, GATE_PIECE)
+        store(0, GATE_PIECE)
+        gate(partial, stream, UNGATED, n)
+        gate(result, partial, GATE_PIECE, UNGATED)
+        look_up(result, partial, UNGATED, n - LAST_PIECE)
+        store(GATE_PIECE, n - LAST_PIECE)
+        look_up(result, partial, n - LAST_PIECE, n)
+        store(n - LAST_PIECE, n)

@@ -7,7 +7,7 @@ MULT = mybir.AluOpType.mult
 P = 128
 ENTRIES_A_COLUMN = 16
 GATE_PIECE = 512
-EARLY = 256
+EARLY = 384
 UNGATED = 704
 LAST_PIECE = 192
 
@@ -49,14 +49,10 @@ def tile_lookup_vg_mulsig_out_kernel(tc, tab, y, offs, out):
             stop = start + GATE_PIECE
             nc.scalar.activation(opened[:, start:stop], gates[:].indirect(entries(offsets, start, stop)), SIGMOID)
 
-        early_halves = ((0, EARLY // 2), (EARLY // 2, EARLY))
-        for start, stop in early_halves:
-            look_up(partial, stream, start, stop)
-        for start, stop in early_halves:
-            gate(result, partial, start, stop)
+        look_up(partial, stream, 0, EARLY)
         look_up(partial, stream, EARLY, GATE_PIECE)
         look_up(partial, stream, GATE_PIECE, UNGATED)
-        gate(result, partial, EARLY, GATE_PIECE)
+        gate(result, partial, 0, GATE_PIECE)
         store(0, GATE_PIECE)
         gate(partial, stream, UNGATED, n)
         gate(result, partial, GATE_PIECE, UNGATED)

@@ -8,7 +8,6 @@ P = 128
 ENTRIES_A_COLUMN = 16
 GATE_PIECE = 512
 EARLY = 384
-UNGATED = 704
 LAST_PIECE = 192
 
 
@@ -51,12 +50,11 @@ def tile_lookup_vg_mulsig_out_kernel(tc, tab, y, offs, out):
 
         look_up(partial, stream, 0, EARLY)
         look_up(partial, stream, EARLY, GATE_PIECE)
-        look_up(partial, stream, GATE_PIECE, UNGATED)
+        look_up(partial, stream, GATE_PIECE, n - LAST_PIECE)
         gate(result, partial, 0, GATE_PIECE)
         store(0, GATE_PIECE)
-        gate(partial, stream, UNGATED, n)
-        gate(result, partial, GATE_PIECE, UNGATED)
-        look_up(result, partial, UNGATED, n - LAST_PIECE)
+        gate(partial, stream, n - LAST_PIECE, n)
+        gate(result, partial, GATE_PIECE, n - LAST_PIECE)
         store(GATE_PIECE, n - LAST_PIECE)
         look_up(result, partial, n - LAST_PIECE, n)
         store(n - LAST_PIECE, n)

@@ -7,8 +7,7 @@ MULT = mybir.AluOpType.mult
 P = 128
 ENTRIES_A_COLUMN = 16
 GATE_PIECE = 512
-EARLY = 384
-LAST_PIECE = 192
+VALUE_PIECES = (384, 320, 192, 128)
 
 
 def entries(offsets, start, stop):
@@ -19,42 +18,30 @@ def tile_lookup_vg_mulsig_out_kernel(tc, tab, y, offs, out):
     nc = tc.nc
     places = tab.shape[2]
     n = y.shape[1]
+    assert sum(VALUE_PIECES) == n
     with tc.tile_pool(name="held", bufs=1) as held:
         offsets = held.tile([P, n // ENTRIES_A_COLUMN], U16)
         gates = held.tile([P, places], F32)
         stream = held.tile([P, n], F32)
         values = held.tile([P, places], F32)
         opened = held.tile([P, n], F32)
-        partial = held.tile([P, n], F32)
+        gated = held.tile([P, n], F32)
         result = held.tile([P, n], F32)
 
-        nc.sync.dma_start(gates[:], tab[1])
+        nc.scalar.dma_start(gates[:], tab[1])
         nc.sync.dma_start(offsets[:], offs)
-        nc.sync.dma_start(stream[:, :EARLY], y[:, :EARLY])
-        nc.sync.dma_start(values[:], tab[0])
-        nc.sync.dma_start(stream[:, EARLY:], y[:, EARLY:])
-
-        def look_up(into, factor, start, stop):
-            looked_up = values[:].indirect(entries(offsets, start, stop))
-            nc.vector.tensor_tensor(into[:, start:stop], looked_up, factor[:, start:stop], MULT)
-
-        def gate(into, factor, start, stop):
-            nc.vector.tensor_tensor(into[:, start:stop], opened[:, start:stop], factor[:, start:stop], MULT)
-
-        def store(start, stop):
-            nc.sync.dma_start(out[:, start:stop], result[:, start:stop])
+        nc.scalar.dma_start(stream[:], y)
+        nc.scalar.dma_start(values[:], tab[0])
 
         for start in range(0, n, GATE_PIECE):
             stop = start + GATE_PIECE
             nc.scalar.activation(opened[:, start:stop], gates[:].indirect(entries(offsets, start, stop)), SIGMOID)
+            nc.vector.tensor_tensor(gated[:, start:stop], opened[:, start:stop], stream[:, start:stop], MULT)
 
-        look_up(partial, stream, 0, EARLY)
-        look_up(partial, stream, EARLY, GATE_PIECE)
-        look_up(partial, stream, GATE_PIECE, n - LAST_PIECE)
-        gate(result, partial, 0, GATE_PIECE)
-        store(0, GATE_PIECE)
-        gate(partial, stream, n - LAST_PIECE, n)
-        gate(result, partial, GATE_PIECE, n - LAST_PIECE)
-        store(GATE_PIECE, n - LAST_PIECE)
-        look_up(result, partial, n - LAST_PIECE, n)
-        store(n - LAST_PIECE, n)
+        start = 0
+        for piece in VALUE_PIECES:
+            stop = start + piece
+            looked_up = values[:].indirect(entries(offsets, start, stop))
+            nc.vector.tensor_tensor(result[:, start:stop], looked_up, gated[:, start:stop], MULT)
+            nc.sync.dma_start(out[:, start:stop], result[:, start:stop])
+            start = stop

@@ -30,8 +30,8 @@ def tile_lookup_vg_mulsig_out_kernel(tc, tab, y, offs, out):
 
         nc.scalar.dma_start(gates[:], tab[1])
         nc.sync.dma_start(offsets[:], offs)
-        nc.scalar.dma_start(stream[:], y)
-        nc.scalar.dma_start(values[:], tab[0])
+        nc.sync.dma_start(stream[:], y)
+        nc.sync.dma_start(values[:], tab[0])
 
         for start in range(0, n, GATE_PIECE):
             stop = start + GATE_PIECE

@@ -7,7 +7,7 @@ MULT = mybir.AluOpType.mult
 P = 128
 ENTRIES_A_COLUMN = 16
 GATE_PIECE = 512
-VALUE_PIECES = (384, 320, 192, 128)
+STORES = ((384, 224), (288,), (128,))
 
 
 def entries(offsets, start, stop):
@@ -18,7 +18,6 @@ def tile_lookup_vg_mulsig_out_kernel(tc, tab, y, offs, out):
     nc = tc.nc
     places = tab.shape[2]
     n = y.shape[1]
-    assert sum(VALUE_PIECES) == n
     with tc.tile_pool(name="held", bufs=1) as held:
         offsets = held.tile([P, n // ENTRIES_A_COLUMN], U16)
         gates = held.tile([P, places], F32)
@@ -39,9 +38,11 @@ def tile_lookup_vg_mulsig_out_kernel(tc, tab, y, offs, out):
             nc.vector.tensor_tensor(gated[:, start:stop], opened[:, start:stop], stream[:, start:stop], MULT)
 
         start = 0
-        for piece in VALUE_PIECES:
-            stop = start + piece
-            looked_up = values[:].indirect(entries(offsets, start, stop))
-            nc.vector.tensor_tensor(result[:, start:stop], looked_up, gated[:, start:stop], MULT)
-            nc.sync.dma_start(out[:, start:stop], result[:, start:stop])
-            start = stop
+        for pieces in STORES:
+            stored_from = start
+            for piece in pieces:
+                stop = start + piece
+                looked_up = values[:].indirect(entries(offsets, start, stop))
+                nc.vector.tensor_tensor(result[:, start:stop], looked_up, gated[:, start:stop], MULT)
+                start = stop
+            nc.sync.dma_start(out[:, stored_from:start], result[:, stored_from:start])

@@ -7,11 +7,20 @@ MULT = mybir.AluOpType.mult
 P = 128
 ENTRIES_A_COLUMN = 16
 GATE_PIECE = 512
-STORES = ((384, 224), (288,), (128,))
+GATINGS = ((512,), (96, 416))
+VALUE_PIECES = (608, 288, 128)
 
 
-def entries(offsets, start, stop):
-    return offsets[:, start // ENTRIES_A_COLUMN : stop // ENTRIES_A_COLUMN]
+def cut(start, pieces):
+    slices = []
+    for piece in pieces:
+        slices.append(slice(start, start + piece))
+        start += piece
+    return slices
+
+
+def entries(offsets, cols):
+    return offsets[:, cols.start // ENTRIES_A_COLUMN : cols.stop // ENTRIES_A_COLUMN]
 
 
 def tile_lookup_vg_mulsig_out_kernel(tc, tab, y, offs, out):
@@ -32,17 +41,11 @@ def tile_lookup_vg_mulsig_out_kernel(tc, tab, y, offs, out):
         nc.sync.dma_start(stream[:], y)
         nc.sync.dma_start(values[:], tab[0])
 
-        for start in range(0, n, GATE_PIECE):
-            stop = start + GATE_PIECE
-            nc.scalar.activation(opened[:, start:stop], gates[:].indirect(entries(offsets, start, stop)), SIGMOID)
-            nc.vector.tensor_tensor(gated[:, start:stop], opened[:, start:stop], stream[:, start:stop], MULT)
+        for half, gatings in zip(cut(0, (GATE_PIECE, GATE_PIECE)), GATINGS):
+            nc.scalar.activation(opened[:, half], gates[:].indirect(entries(offsets, half)), SIGMOID)
+            for cols in cut(half.start, gatings):
+                nc.vector.tensor_tensor(gated[:, cols], opened[:, cols], stream[:, cols], MULT)
 
-        start = 0
-        for pieces in STORES:
-            stored_from = start
-            for piece in pieces:
-                stop = start + piece
-                looked_up = values[:].indirect(entries(offsets, start, stop))
-                nc.vector.tensor_tensor(result[:, start:stop], looked_up, gated[:, start:stop], MULT)
-                start = stop
-            nc.sync.dma_start(out[:, stored_from:start], result[:, stored_from:start])
+        for cols in cut(0, VALUE_PIECES):
+            nc.vector.tensor_tensor(result[:, cols], values[:].indirect(entries(offsets, cols)), gated[:, cols], MULT)
+            nc.sync.dma_start(out[:, cols], result[:, cols])

@@ -7,8 +7,7 @@ MULT = mybir.AluOpType.mult
 P = 128
 ENTRIES_A_COLUMN = 16
 GATE_PIECE = 512
-GATINGS = ((512,), (96, 416))
-VALUE_PIECES = (608, 288, 128)
+VALUE_PIECES = (512, 320, 192)
 
 
 def cut(start, pieces):
@@ -41,10 +40,9 @@ def tile_lookup_vg_mulsig_out_kernel(tc, tab, y, offs, out):
         nc.sync.dma_start(stream[:], y)
         nc.sync.dma_start(values[:], tab[0])
 
-        for half, gatings in zip(cut(0, (GATE_PIECE, GATE_PIECE)), GATINGS):
+        for half in cut(0, (GATE_PIECE, GATE_PIECE)):
             nc.scalar.activation(opened[:, half], gates[:].indirect(entries(offsets, half)), SIGMOID)
-            for cols in cut(half.start, gatings):
-                nc.vector.tensor_tensor(gated[:, cols], opened[:, cols], stream[:, cols], MULT)
+            nc.vector.tensor_tensor(gated[:, half], opened[:, half], stream[:, half], MULT)
 
         for cols in cut(0, VALUE_PIECES):
             nc.vector.tensor_tensor(result[:, cols], values[:].indirect(entries(offsets, cols)), gated[:, cols], MULT)

import concourse.mybir as mybir

F32, U16 = mybir.dt.float32, mybir.dt.uint16
SIGMOID = mybir.ActivationFunctionType.Sigmoid
MULT = mybir.AluOpType.mult

P = 128
ENTRIES_A_COLUMN = 16
GATE_PIECE = 512
VALUE_PIECES = (512, 320, 192)


def cut(start, pieces):
    slices = []
    for piece in pieces:
        slices.append(slice(start, start + piece))
        start += piece
    return slices


def entries(offsets, cols):
    return offsets[:, cols.start // ENTRIES_A_COLUMN : cols.stop // ENTRIES_A_COLUMN]


def tile_lookup_vg_mulsig_out_kernel(tc, tab, y, offs, out):
    nc = tc.nc
    places = tab.shape[2]
    n = y.shape[1]
    with tc.tile_pool(name="held", bufs=1) as held:
        offsets = held.tile([P, n // ENTRIES_A_COLUMN], U16)
        gates = held.tile([P, places], F32)
        stream = held.tile([P, n], F32)
        values = held.tile([P, places], F32)
        opened = held.tile([P, n], F32)
        gated = held.tile([P, n], F32)
        result = held.tile([P, n], F32)

        nc.scalar.dma_start(gates[:], tab[1])
        nc.sync.dma_start(offsets[:], offs)
        nc.sync.dma_start(stream[:], y)
        nc.sync.dma_start(values[:], tab[0])

        for half in cut(0, (GATE_PIECE, GATE_PIECE)):
            nc.scalar.activation(opened[:, half], gates[:].indirect(entries(offsets, half)), SIGMOID)
            nc.vector.tensor_tensor(gated[:, half], opened[:, half], stream[:, half], MULT)

        for cols in cut(0, VALUE_PIECES):
            nc.vector.tensor_tensor(result[:, cols], values[:].indirect(entries(offsets, cols)), gated[:, cols], MULT)
            nc.sync.dma_start(out[:, cols], result[:, cols])
